import numpy as np
import ml_dtypes

BF16 = ml_dtypes.bfloat16


def bf(x):
    return np.asarray(x, np.float32).astype(BF16)


def f32(x):
    return np.asarray(x, np.float32)


def f64(x):
    return np.asarray(x).astype(np.float64)


def striped(idx):
    return np.tile(idx.reshape(-1, 16).T, (8, 1))


S, K, M, N, E, Q = 256, 256, 128, 192, 2, 96


def setup_inputs():
    return {"base": bf(np.random.standard_normal((M, S))), "x": bf(np.random.standard_normal((K, N))), "w": bf(np.random.standard_normal((E, K, M)) / np.sqrt(K)), "b": f32(0.5 * np.random.standard_normal((M, 1))), "offs": striped(np.random.permutation(S)[:N])}


def reference(base, x, w, b, offs):
    idx = offs[:16].T.reshape(-1)
    z = f64(base).copy()
    for e in range(E):
        z[:, idx[e * Q : (e + 1) * Q]] += f64(w)[e].T @ f64(x)[:, e * Q : (e + 1) * Q]
    return np.maximum(z + f64(b), 0.0)

@@ -1,0 +1,58 @@
+import concourse.mybir as mybir
+from concourse.masks import make_identity
+
+P = 128
+TOKENS = 256
+ENTRIES = 192
+EXPERTS = 2
+PIECE = ENTRIES // EXPERTS
+K_BLOCKS = 256 // P
+PIECE_COLS = PIECE // 16
+
+FLOPS = 2 * 256 * P * ENTRIES
+
+BF16, F32, U16 = mybir.dt.bfloat16, mybir.dt.float32, mybir.dt.uint16
+ADD, MAX = mybir.AluOpType.add, mybir.AluOpType.max
+
+
+def tile_scatter_matmul_kernel(tc, base, x, w, b, offs, out):
+    nc = tc.nc
+    with (
+        tc.tile_pool(name="held", bufs=1) as held,
+        tc.psum_pool(name="psum", bufs=1) as psum,
+    ):
+        offsets = held.tile([P, ENTRIES // 16], U16, name="offsets")
+        nc.sync.dma_start(offsets[:], offs)
+
+        base_tile = held.tile([P, TOKENS], BF16, name="base_tile")
+        nc.scalar.dma_start(base_tile[:], base)
+
+        x_tile = held.tile([P, K_BLOCKS, ENTRIES], BF16, name="x_tile")
+        nc.sync.dma_start(x_tile[:], x.rearrange("(a p) n -> p a n", p=P))
+        w_tile = held.tile([P, EXPERTS * K_BLOCKS, P], BF16, name="w_tile")
+        nc.scalar.dma_start(w_tile[:], w.flatten_outer_dims().rearrange("(c p) m -> p c m", p=P))
+
+        bias = held.tile([P, 1], F32, name="bias")
+        nc.sync.dma_start(bias[:], b)
+
+        identity = held.tile([P, P], BF16, name="identity")
+        make_identity(nc, identity[:])
+
+        window = psum.tile([P, TOKENS], F32, name="window")
+        nc.tensor.matmul(window[:], identity[:], base_tile[:], start=True, stop=False)
+
+        for e in range(EXPERTS):
+            places = offsets[:, e * PIECE_COLS : (e + 1) * PIECE_COLS]
+            for a in range(K_BLOCKS):
+                last = e == EXPERTS - 1 and a == K_BLOCKS - 1
+                nc.tensor.matmul(
+                    window[:].indirect(places),
+                    w_tile[:, e * K_BLOCKS + a, :],
+                    x_tile[:, a, e * PIECE : (e + 1) * PIECE],
+                    start=False,
+                    stop=last,
+                )
+
+        result = held.tile([P, TOKENS], F32, name="result")
+        nc.vector.tensor_scalar(result[:], window[:], bias[:, 0:1], 0.0, ADD, MAX)
+        nc.sync.dma_start(out, result[:])

@@ -28,12 +28,16 @@ def tile_scatter_matmul_kernel(tc, base, x, w, b, offs, out):
         nc.scalar.dma_start(base_tile[:], base)
 
         x_tile = held.tile([P, K_BLOCKS, ENTRIES], BF16, name="x_tile")
-        nc.sync.dma_start(x_tile[:], x.rearrange("(a p) n -> p a n", p=P))
-        w_tile = held.tile([P, EXPERTS * K_BLOCKS, P], BF16, name="w_tile")
-        nc.scalar.dma_start(w_tile[:], w.flatten_outer_dims().rearrange("(c p) m -> p c m", p=P))
+        nc.sync.dma_start(x_tile[:], x.rearrange("(p a) n -> p a n", a=K_BLOCKS))
+        w_tiles = []
+        for e in range(EXPERTS):
+            w_tile = held.tile([P, K_BLOCKS, P], BF16, name="w_tile%d" % e)
+            queue = nc.scalar if e % 2 == 0 else nc.sync
+            queue.dma_start(w_tile[:], w[e].rearrange("(p a) m -> p a m", a=K_BLOCKS))
+            w_tiles.append(w_tile)
 
         bias = held.tile([P, 1], F32, name="bias")
-        nc.sync.dma_start(bias[:], b)
+        nc.scalar.dma_start(bias[:], b)
 
         identity = held.tile([P, P], BF16, name="identity")
         make_identity(nc, identity[:])
@@ -47,7 +51,7 @@ def tile_scatter_matmul_kernel(tc, base, x, w, b, offs, out):
                 last = e == EXPERTS - 1 and a == K_BLOCKS - 1
                 nc.tensor.matmul(
                     window[:].indirect(places),
-                    w_tile[:, e * K_BLOCKS + a, :],
+                    w_tiles[e][:, a, :],
                     x_tile[:, a, e * PIECE : (e + 1) * PIECE],
                     start=False,
                     stop=last,

@@ -9,6 +9,8 @@ PIECE = ENTRIES // EXPERTS
 K_BLOCKS = 256 // P
 PIECE_COLS = PIECE // 16
 
+WARM_UPS = 12
+
 FLOPS = 2 * 256 * P * ENTRIES
 
 BF16, F32, U16 = mybir.dt.bfloat16, mybir.dt.float32, mybir.dt.uint16
@@ -21,6 +23,12 @@ def tile_scatter_matmul_kernel(tc, base, x, w, b, offs, out):
         tc.tile_pool(name="held", bufs=1) as held,
         tc.psum_pool(name="psum", bufs=1) as psum,
     ):
+        zeros = held.tile([P, P], BF16, name="zeros")
+        nc.gpsimd.memset(zeros[:], 0.0)
+        unread = psum.tile([P, P], F32, name="unread")
+        for _ in range(WARM_UPS):
+            nc.tensor.matmul(unread[:], zeros[:], zeros[:], start=True, stop=True)
+
         offsets = held.tile([P, ENTRIES // 16], U16, name="offsets")
         nc.sync.dma_start(offsets[:], offs)
 

@@ -9,6 +9,8 @@ PIECE = ENTRIES // EXPERTS
 K_BLOCKS = 256 // P
 PIECE_COLS = PIECE // 16
 
+BLOCK = 32
+
 WARM_UPS = 12
 
 FLOPS = 2 * 256 * P * ENTRIES
@@ -23,6 +25,9 @@ def tile_scatter_matmul_kernel(tc, base, x, w, b, offs, out):
         tc.tile_pool(name="held", bufs=1) as held,
         tc.psum_pool(name="psum", bufs=1) as psum,
     ):
+        bias_rows = held.tile([P, BLOCK], F32, name="bias_rows")
+        bias_cols = held.tile([P, BLOCK], F32, name="bias_cols")
+
         zeros = held.tile([P, P], BF16, name="zeros")
         nc.gpsimd.memset(zeros[:], 0.0)
         unread = psum.tile([P, P], F32, name="unread")
@@ -44,8 +49,9 @@ def tile_scatter_matmul_kernel(tc, base, x, w, b, offs, out):
             queue.dma_start(w_tile[:], w[e].rearrange("(p a) m -> p a m", a=K_BLOCKS))
             w_tiles.append(w_tile)
 
-        bias = held.tile([P, 1], F32, name="bias")
-        nc.scalar.dma_start(bias[:], b)
+        nc.vector.memset(bias_rows[:], 0.0)
+        nc.scalar.dma_start(bias_rows[0:P:BLOCK, :], b.rearrange("(g c) o -> g (c o)", c=BLOCK))
+        nc.vector.transpose(bias_cols[:], bias_rows[:])
 
         identity = held.tile([P, P], BF16, name="identity")
         make_identity(nc, identity[:])
@@ -66,5 +72,5 @@ def tile_scatter_matmul_kernel(tc, base, x, w, b, offs, out):
                 )
 
         result = held.tile([P, TOKENS], F32, name="result")
-        nc.vector.tensor_scalar(result[:], window[:], bias[:, 0:1], 0.0, ADD, MAX)
+        nc.vector.tensor_scalar(result[:], window[:], bias_cols[:, 0:1], 0.0, ADD, MAX)
         nc.sync.dma_start(out, result[:])

@@ -11,7 +11,8 @@ PIECE_COLS = PIECE // 16
 
 BLOCK = 32
 
-WARM_UPS = 12
+WARM_UPS = 3
+WARM_COLS = 512
 
 FLOPS = 2 * 256 * P * ENTRIES
 
@@ -28,11 +29,17 @@ def tile_scatter_matmul_kernel(tc, base, x, w, b, offs, out):
         bias_rows = held.tile([P, BLOCK], F32, name="bias_rows")
         bias_cols = held.tile([P, BLOCK], F32, name="bias_cols")
 
-        zeros = held.tile([P, P], BF16, name="zeros")
+        zeros = held.tile([P, 2], BF16, name="zeros")
         nc.gpsimd.memset(zeros[:], 0.0)
-        unread = psum.tile([P, P], F32, name="unread")
+        unread = psum.tile([P, WARM_COLS], F32, name="unread")
         for _ in range(WARM_UPS):
-            nc.tensor.matmul(unread[:], zeros[:], zeros[:], start=True, stop=True)
+            nc.tensor.matmul(
+                unread[:],
+                zeros[:, 0:1].to_broadcast([P, P]),
+                zeros[:, 0:1].to_broadcast([P, WARM_COLS]),
+                start=True,
+                stop=True,
+            )
 
         offsets = held.tile([P, ENTRIES // 16], U16, name="offsets")
         nc.sync.dma_start(offsets[:], offs)

@@ -9,6 +9,7 @@ PIECE = ENTRIES // EXPERTS
 K_BLOCKS = 256 // P
 PIECE_COLS = PIECE // 16
 
+BURST = 256
 BLOCK = 32
 
 WARM_UPS = 3
@@ -44,14 +45,14 @@ def tile_scatter_matmul_kernel(tc, base, x, w, b, offs, out):
         offsets = held.tile([P, ENTRIES // 16], U16, name="offsets")
         nc.sync.dma_start(offsets[:], offs)
 
-        base_tile = held.tile([P, TOKENS], BF16, name="base_tile")
+        base_tile = held.tile([P, TOKENS], BF16, name="base_tile", align_bytes=BURST)
         nc.scalar.dma_start(base_tile[:], base)
 
-        x_tile = held.tile([P, K_BLOCKS, ENTRIES], BF16, name="x_tile")
+        x_tile = held.tile([P, K_BLOCKS, ENTRIES], BF16, name="x_tile", align_bytes=BURST)
         nc.sync.dma_start(x_tile[:], x.rearrange("(p a) n -> p a n", a=K_BLOCKS))
         w_tiles = []
         for e in range(EXPERTS):
-            w_tile = held.tile([P, K_BLOCKS, P], BF16, name="w_tile%d" % e)
+            w_tile = held.tile([P, K_BLOCKS, P], BF16, name="w_tile%d" % e, align_bytes=BURST)
             queue = nc.scalar if e % 2 == 0 else nc.sync
             queue.dma_start(w_tile[:], w[e].rearrange("(p a) m -> p a m", a=K_BLOCKS))
             w_tiles.append(w_tile)
@@ -78,6 +79,6 @@ def tile_scatter_matmul_kernel(tc, base, x, w, b, offs, out):
                     stop=last,
                 )
 
-        result = held.tile([P, TOKENS], F32, name="result")
+        result = held.tile([P, TOKENS], F32, name="result", align_bytes=BURST)
         nc.vector.tensor_scalar(result[:], window[:], bias_cols[:, 0:1], 0.0, ADD, MAX)
         nc.sync.dma_start(out, result[:])

@@ -58,7 +58,7 @@ def tile_scatter_matmul_kernel(tc, base, x, w, b, offs, out):
             w_tiles.append(w_tile)
 
         nc.vector.memset(bias_rows[:], 0.0)
-        nc.scalar.dma_start(bias_rows[0:P:BLOCK, :], b.rearrange("(g c) o -> g (c o)", c=BLOCK))
+        nc.sync.dma_start(bias_rows[0:P:BLOCK, :], b.rearrange("(g c) o -> g (c o)", c=BLOCK))
         nc.vector.transpose(bias_cols[:], bias_rows[:])
 
         identity = held.tile([P, P], BF16, name="identity")

@@ -81,4 +81,4 @@ def tile_scatter_matmul_kernel(tc, base, x, w, b, offs, out):
 
         result = held.tile([P, TOKENS], F32, name="result", align_bytes=BURST)
         nc.vector.tensor_scalar(result[:], window[:], bias_cols[:, 0:1], 0.0, ADD, MAX)
-        nc.sync.dma_start(out, result[:])
+        nc.sync.dma_start(out, result[:], max_dma_last_dim=512)

import concourse.mybir as mybir
from concourse.masks import make_identity

P = 128
TOKENS = 256
ENTRIES = 192
EXPERTS = 2
PIECE = ENTRIES // EXPERTS
K_BLOCKS = 256 // P
PIECE_COLS = PIECE // 16

BURST = 256
BLOCK = 32

WARM_UPS = 3
WARM_COLS = 512

FLOPS = 2 * 256 * P * ENTRIES

BF16, F32, U16 = mybir.dt.bfloat16, mybir.dt.float32, mybir.dt.uint16
ADD, MAX = mybir.AluOpType.add, mybir.AluOpType.max


def tile_scatter_matmul_kernel(tc, base, x, w, b, offs, out):
    nc = tc.nc
    with (
        tc.tile_pool(name="held", bufs=1) as held,
        tc.psum_pool(name="psum", bufs=1) as psum,
    ):
        bias_rows = held.tile([P, BLOCK], F32, name="bias_rows")
        bias_cols = held.tile([P, BLOCK], F32, name="bias_cols")

        zeros = held.tile([P, 2], BF16, name="zeros")
        nc.gpsimd.memset(zeros[:], 0.0)
        unread = psum.tile([P, WARM_COLS], F32, name="unread")
        for _ in range(WARM_UPS):
            nc.tensor.matmul(
                unread[:],
                zeros[:, 0:1].to_broadcast([P, P]),
                zeros[:, 0:1].to_broadcast([P, WARM_COLS]),
                start=True,
                stop=True,
            )

        offsets = held.tile([P, ENTRIES // 16], U16, name="offsets")
        nc.sync.dma_start(offsets[:], offs)

        base_tile = held.tile([P, TOKENS], BF16, name="base_tile", align_bytes=BURST)
        nc.scalar.dma_start(base_tile[:], base)

        x_tile = held.tile([P, K_BLOCKS, ENTRIES], BF16, name="x_tile", align_bytes=BURST)
        nc.sync.dma_start(x_tile[:], x.rearrange("(p a) n -> p a n", a=K_BLOCKS))
        w_tiles = []
        for e in range(EXPERTS):
            w_tile = held.tile([P, K_BLOCKS, P], BF16, name="w_tile%d" % e, align_bytes=BURST)
            queue = nc.scalar if e % 2 == 0 else nc.sync
            queue.dma_start(w_tile[:], w[e].rearrange("(p a) m -> p a m", a=K_BLOCKS))
            w_tiles.append(w_tile)

        nc.vector.memset(bias_rows[:], 0.0)
        nc.sync.dma_start(bias_rows[0:P:BLOCK, :], b.rearrange("(g c) o -> g (c o)", c=BLOCK))
        nc.vector.transpose(bias_cols[:], bias_rows[:])

        identity = held.tile([P, P], BF16, name="identity")
        make_identity(nc, identity[:])

        window = psum.tile([P, TOKENS], F32, name="window")
        nc.tensor.matmul(window[:], identity[:], base_tile[:], start=True, stop=False)

        for e in range(EXPERTS):
            places = offsets[:, e * PIECE_COLS : (e + 1) * PIECE_COLS]
            for a in range(K_BLOCKS):
                last = e == EXPERTS - 1 and a == K_BLOCKS - 1
                nc.tensor.matmul(
                    window[:].indirect(places),
                    w_tiles[e][:, a, :],
                    x_tile[:, a, e * PIECE : (e + 1) * PIECE],
                    start=False,
                    stop=last,
                )

        result = held.tile([P, TOKENS], F32, name="result", align_bytes=BURST)
        nc.vector.tensor_scalar(result[:], window[:], bias_cols[:, 0:1], 0.0, ADD, MAX)
        nc.sync.dma_start(out, result[:], max_dma_last_dim=512)
